import numpy as np
import ml_dtypes


def mxq(x, axis, fmt="e4m3"):
    dtype, down = {"e4m3": (ml_dtypes.float8_e4m3fn, 7), "e5m2": (ml_dtypes.float8_e5m2, 14)}[fmt]
    v = np.moveaxis(np.asarray(x, np.float32).astype(ml_dtypes.bfloat16).astype(np.float64), axis, -1)
    blocks = v.reshape(v.shape[:-1] + (-1, 32))
    amax = np.abs(blocks).max(-1, keepdims=True)
    byte = np.maximum(np.where(amax > 0, np.frexp(amax)[1] - 1 + 127, 0) - down, 1)
    scale = np.exp2(byte - 127.0)
    codes = (blocks / scale).astype(np.float32).astype(dtype).astype(np.float64)
    return np.moveaxis((codes * scale).reshape(v.shape), -1, axis)


WIDE = False


def mx_kscale(k):
    if not WIDE:
        return np.ones(k)
    levels = np.array([10, -10, 5, -5, 0])
    if k % 512:
        return np.exp2(np.random.permutation(np.resize(levels, k // 32))).repeat(32)
    a = np.empty((k // 512, 16))
    for p in range(k // 512):
        a[p, :8] = np.random.permutation(np.resize(levels, 8))
        for g in range(8):
            far = levels[np.abs(levels - a[p, g]) >= 10]
            a[p, g + 8] = far[np.random.randint(len(far))]
    return np.exp2(a.ravel()).repeat(32)


def f64(x):
    return np.asarray(x).astype(np.float64)


def striped(idx):
    return np.tile(idx.reshape(-1, 16).T, (8, 1)).astype(np.uint16)


def unstriped(offs):
    return offs[:16].T.reshape(-1).astype(np.int64)


E2M1 = np.array([0.0, 0.5, 1.0, 1.5, 2.0, 3.0, 4.0, 6.0, -0.0, -0.5, -1.0, -1.5, -2.0, -3.0, -4.0, -6.0])


def pack_weight(w, fmt):
    k, n = w.shape
    w = f64(np.asarray(w, np.float32).astype(ml_dtypes.bfloat16)).reshape(k // 32, 32, n)
    amax = np.abs(w).max(1)
    if fmt == "e4m3":
        byte = np.frexp(amax)[1] - 1 + 127 - 7
    else:
        mant, ex = np.frexp(amax / 6.0)
        byte = np.where(mant > 0.5, ex, ex - 1) + 127
    byte = np.clip(np.where(amax > 0, byte, 1), 1, 254)
    scaled = (w * np.exp2(127.0 - byte)[:, None, :]).reshape(k, n).astype(np.float32)
    by_word = np.ascontiguousarray(scaled.reshape(k // 512, 128, 4, n).transpose(0, 1, 3, 2))
    if fmt == "e4m3":
        words = by_word.astype(ml_dtypes.float8_e4m3fn).view(np.uint8)
    else:
        c = by_word.astype(ml_dtypes.float4_e2m1fn).view(np.uint8) & 0xF
        words = (c[..., 0::2] | (c[..., 1::2] << 4)).reshape(k // 512, 128, 2 * n)
    return np.ascontiguousarray(words), np.ascontiguousarray(byte.astype(np.uint8).reshape(k // 512, 16, n))


def unpack_weight(words, scales, fmt):
    g, _, n = scales.shape
    words = np.ascontiguousarray(words).reshape(g, 128, n, -1)
    if fmt == "e4m3":
        vals = words.view(ml_dtypes.float8_e4m3fn).astype(np.float64)
    else:
        nib = np.empty((g, 128, n, 4), np.uint8)
        nib[..., 0::2] = words & 0xF
        nib[..., 1::2] = words >> 4
        vals = E2M1[nib]
    vals = vals * np.repeat(np.exp2(scales.astype(np.float64) - 127.0), 8, axis=1)[..., None]
    return vals.transpose(0, 1, 3, 2).reshape(g * 512, n)


def silu(v):
    return v / (1.0 + np.exp(-np.maximum(v, -700.0)))


K, M, T, S = 1536, 256, 4096, 2048


def setup_inputs():
    n = np.random.standard_normal
    s = mx_kscale(K)[:, None]
    u = mx_kscale(512)[:, None]
    v = pack_weight(n((K, T)) * s, "e4m3")
    p_w2 = pack_weight(1.4 * n((512, M)) / np.sqrt(512) / u, "e2m1")
    return {
        "tab_words": v[0],
        "tab_scales": v[1],
        "w1": (n((K, 512)) / np.sqrt(K) / s * u.T).astype(np.float32),
        "w2_words": p_w2[0],
        "w2_scales": p_w2[1],
        "ts": np.tile(np.exp(0.5 * n(T)), (128, 1)).astype(np.float32),
        "b": (0.3 * n(256)).astype(np.float32),
        "offs": striped(np.random.permutation(T)[:S]),
    }


def reference(tab_words, tab_scales, w1, w2_words, w2_scales, ts, b, offs):
    tab_ = unpack_weight(tab_words, tab_scales, "e4m3")[:, unstriped(offs)]
    w1_ = mxq(f64(w1), 0, "e4m3")
    w2_ = unpack_weight(w2_words, w2_scales, "e2m1")
    h_ = mxq(np.maximum(w1_.T @ tab_, 0.0), 0, "e4m3")
    y = w2_.T @ h_
    y = y * f64(ts)[0][unstriped(offs)]
    return silu(y + f64(b)[:, None])

@@ -1,0 +1,215 @@
+from contextlib import ExitStack
+
+import concourse.mybir as mybir
+from concourse.masks import make_identity
+
+K, H, M, T, S = 1536, 512, 256, 4096, 2048
+FLOPS = 2 * K * H * S + 2 * H * M * S
+
+F32 = mybir.dt.float32
+BF16 = mybir.dt.bfloat16
+I32 = mybir.dt.int32
+U32 = mybir.dt.uint32
+U16 = mybir.dt.uint16
+U8 = mybir.dt.uint8
+FP8X4 = mybir.dt.float8_e4m3fn_x4
+FP4X4 = mybir.dt.float4_e2m1fn_x4
+ACT = mybir.ActivationFunctionType
+ALU = mybir.AluOpType
+
+P = 128
+PACK = 4
+PASSES = K // (P * PACK)
+BANK = 128
+GROUP = 256
+GROUPS = S // GROUP
+TS_SLICE = 256
+AHEAD = 2
+
+
+def tile_list_tabts_silu_kernel(
+    tc, tab_words, tab_scales, w1, w2_words, w2_scales, ts, b, offs, out
+):
+    nc = tc.nc
+    with ExitStack() as ctx:
+        keep = ctx.enter_context(tc.tile_pool(name="keep", bufs=1))
+        ring = ctx.enter_context(tc.tile_pool(name="ring", bufs=3))
+        psum = ctx.enter_context(tc.psum_pool(name="psum", bufs=8))
+
+        offsets = keep.tile([P, S // 16], U16, name="offsets")
+        nc.sync.dma_start(offsets[:], offs)
+
+        def entries(first, count):
+            return offsets[:, first // 16 : (first + count) // 16]
+
+        scale_window = keep.tile([P, T], U8, name="scale_window", align_bytes=64)
+        w2_plane = keep.tile([P, M], U8, name="w2_plane", align_bytes=64)
+        nc.vector.memset(scale_window[:].bitcast(I32), 0)
+        nc.vector.memset(w2_plane[:].bitcast(I32), 0)
+        for q in range(4):
+            nc.gpsimd.dma_start(
+                out=scale_window[32 * q : 32 * q + 4 * PASSES, :].bitcast(I32),
+                in_=tab_scales[:, 4 * q : 4 * q + 4, :].bitcast(I32),
+            )
+        ts_rows = keep.tile([P, T // P], F32, name="ts_rows", tag="slot_c", align_bytes=64)
+        nc.scalar.dma_start(out=ts_rows[:], in_=ts[0].rearrange("(p c) -> p c", p=P))
+
+        word_windows = {}
+        w1_raw = {}
+
+        def load_words(a, tag):
+            window = keep.tile([P, T], I32, name="word_window%d" % a, tag=tag, align_bytes=64)
+            nc.sync.dma_start(out=window[:], in_=tab_words[a].rearrange("p t i -> p (t i)").bitcast(I32))
+            word_windows[a] = window
+
+        def load_w1(a, tag):
+            raw = keep.tile([P, PACK, H], F32, name="w1_raw%d" % a, tag=tag, align_bytes=64)
+            rows = w1[a * P * PACK : (a + 1) * P * PACK, :]
+            nc.sync.dma_start(out=raw[:], in_=rows.rearrange("(p j) c -> p j c", j=PACK))
+            w1_raw[a] = raw
+
+        load_words(0, "slot_a")
+        load_w1(0, "slot_b")
+        load_w1(1, "slot_d")
+
+        identity = keep.tile([P, P], F32, name="identity")
+        make_identity(nc, identity[:])
+
+        w2_codes = keep.tile([P, 2 * M], U8, name="w2_codes", align_bytes=64)
+        bias = keep.tile([P, M // P], F32, name="bias")
+        nc.scalar.dma_start(out=w2_codes[:].bitcast(I32), in_=w2_words[0].bitcast(I32))
+        for q in range(4):
+            nc.gpsimd.dma_start(
+                out=w2_plane[32 * q : 32 * q + 4, :].bitcast(I32),
+                in_=w2_scales[0, 4 * q : 4 * q + 4, :].bitcast(I32),
+            )
+        with nc.allow_non_contiguous_dma(reason="one bias value a partition"):
+            nc.scalar.dma_start(out=bias[:], in_=b.rearrange("(u p) -> p u", p=P))
+
+        tab_planes = keep.tile([P, S], U8, name="tab_planes", align_bytes=64)
+        nc.vector.tensor_copy(tab_planes[:], scale_window[:].indirect(offsets[:]))
+
+        ts_window = keep.tile([P, T], F32, name="ts_window", align_bytes=64)
+        ts_view = ts_window[:].rearrange("p (n c) -> p n c", n=P)
+        for c0 in range(0, T // P, 4):
+            spread = psum.tile([P, 4, P], F32, name="spread", tag="bank")
+            for i in range(4):
+                nc.tensor.transpose(
+                    spread[:, i, :], ts_rows[:, c0 + i : c0 + i + 1].to_broadcast([P, P]), identity[:]
+                )
+            nc.scalar.copy(out=ts_view[:, :, c0 : c0 + 4], in_=spread[:].rearrange("p i n -> p n i"))
+
+        w1_codes = []
+        w1_planes = []
+
+        def quantise_w1(a, tag):
+            grouped = keep.tile([P, PACK * H], BF16, name="w1_grouped%d" % a, tag=tag, align_bytes=64)
+            nc.scalar.copy(
+                out=grouped[:].rearrange("p (t m j) -> p m j t", t=PACK, j=PACK),
+                in_=w1_raw[a][:].rearrange("p j (m t) -> p m j t", t=PACK),
+            )
+            codes = keep.tile([P, H], U32, name="w1_codes%d" % a, align_bytes=64)
+            plane = keep.tile([P, H], U8, name="w1_plane%d" % a, align_bytes=64)
+            nc.vector.quantize_mx(out=codes[:].bitcast(FP8X4), scales=plane[:], in_=grouped[:])
+            w1_codes.append(codes)
+            w1_planes.append(plane)
+
+        early_words = {}
+
+        def gather_early(a):
+            for half in range(2):
+                words = keep.tile([P, S // 2], U32, name="early_words%d_%d" % (a, half), align_bytes=64)
+                nc.vector.tensor_copy(
+                    words[:], word_windows[a][:].bitcast(U32).indirect(entries(half * S // 2, S // 2))
+                )
+                early_words[(a, half)] = words
+
+        load_words(1, "slot_c")
+        gather_early(0)
+        quantise_w1(0, "g0")
+        load_w1(2, "slot_b")
+        quantise_w1(1, "g1")
+        load_words(2, "slot_d")
+        gather_early(1)
+        quantise_w1(2, "g2")
+
+        h_tiles = {}
+        ts_slices = {}
+
+        def gather_ts(n):
+            picked = ring.tile([P, TS_SLICE], F32, name="ts_picked", bufs=2)
+            nc.vector.tensor_copy(picked[:], ts_window[:].indirect(entries(n * TS_SLICE, TS_SLICE)))
+            ts_slices[n] = picked
+
+        def first_product(g):
+            last_words = ring.tile([P, GROUP], U32, name="last_words", bufs=4, align_bytes=64)
+            nc.vector.tensor_copy(
+                last_words[:], word_windows[PASSES - 1][:].bitcast(U32).indirect(entries(g * GROUP, GROUP))
+            )
+            h_bf16 = ring.tile([P, GROUP, PACK], BF16, name="h_bf16", bufs=4, align_bytes=64)
+            for half in range(GROUP // BANK):
+                first = g * GROUP + half * BANK
+                h_sums = psum.tile([P, PACK, BANK], F32, name="h_sums", tag="bank")
+                for a in range(PASSES):
+                    if a < PASSES - 1:
+                        place = first % (S // 2)
+                        words = early_words[(a, first // (S // 2))][:, place : place + BANK]
+                    else:
+                        words = last_words[:, half * BANK : (half + 1) * BANK]
+                    for t in range(PACK):
+                        nc.tensor.matmul_mx(
+                            out=h_sums[:, t, :],
+                            lhsT=w1_codes[a][:, t * P : (t + 1) * P].bitcast(FP8X4),
+                            lhsT_scale=w1_planes[a][:, t * P : (t + 1) * P],
+                            rhs=words.bitcast(FP8X4),
+                            rhs_scale=tab_planes[4 * a : P, first : first + BANK],
+                            start=(a == 0 and t == 0),
+                            stop=(a == PASSES - 1 and t == PACK - 1),
+                        )
+                nc.scalar.activation(
+                    out=h_bf16[:, half * BANK : (half + 1) * BANK, :],
+                    in_=h_sums[:].rearrange("p t n -> p n t"),
+                    func=ACT.Relu,
+                )
+            h_tiles[g] = h_bf16
+
+        def second_product(g):
+            h_codes = ring.tile([P, GROUP], U32, name="h_codes", align_bytes=64)
+            h_plane = ring.tile([P, GROUP], U8, name="h_plane", align_bytes=64)
+            nc.vector.quantize_mx(
+                out=h_codes[:].bitcast(FP8X4), scales=h_plane[:], in_=h_tiles[g][:].rearrange("p n t -> p (n t)")
+            )
+            y_sums = psum.tile([P, M // P, GROUP], F32, name="y_sums", tag="bank")
+            for u in range(M // P):
+                nc.tensor.matmul_mx(
+                    out=y_sums[:, u, :],
+                    lhsT=w2_codes[:, 2 * P * u : 2 * P * (u + 1)].bitcast(FP4X4),
+                    lhsT_scale=w2_plane[:, P * u : P * (u + 1)],
+                    rhs=h_codes[:].bitcast(FP8X4),
+                    rhs_scale=h_plane[:],
+                    start=True,
+                    stop=True,
+                )
+            first = (g * GROUP) % TS_SLICE
+            picked = ts_slices[g * GROUP // TS_SLICE][:, first : first + GROUP]
+            scaled = ring.tile([P, M // P, GROUP], F32, name="scaled")
+            nc.vector.tensor_tensor(
+                scaled[:], y_sums[:], picked.unsqueeze(1).to_broadcast([P, M // P, GROUP]), ALU.mult
+            )
+            result = ring.tile([P, M // P, GROUP], F32, name="result")
+            for u in range(M // P):
+                nc.scalar.activation(out=result[:, u, :], in_=scaled[:, u, :], func=ACT.Silu, bias=bias[:, u : u + 1])
+            nc.sync.dma_start(
+                out=out.rearrange("(u p) j -> p u j", p=P)[:, :, g * GROUP : (g + 1) * GROUP], in_=result[:]
+            )
+
+        gather_ts(0)
+        gather_ts(1)
+        for g in range(AHEAD):
+            first_product(g)
+        for g in range(GROUPS):
+            if g + AHEAD < GROUPS:
+                first_product(g + AHEAD)
+            second_product(g)
+            if g + 2 < GROUPS:
+                gather_ts(g + 2)

@@ -24,6 +24,7 @@ BANK = 128
 GROUP = 256
 GROUPS = S // GROUP
 TS_SLICE = 256
+TS_SPLIT = 24
 AHEAD = 2
 
 
@@ -51,8 +52,12 @@ def tile_list_tabts_silu_kernel(
                 out=scale_window[32 * q : 32 * q + 4 * PASSES, :].bitcast(I32),
                 in_=tab_scales[:, 4 * q : 4 * q + 4, :].bitcast(I32),
             )
-        ts_rows = keep.tile([P, T // P], F32, name="ts_rows", tag="slot_c", align_bytes=64)
-        nc.scalar.dma_start(out=ts_rows[:], in_=ts[0].rearrange("(p c) -> p c", p=P))
+        ts_columns = {}
+        for first, count, tag in ((0, TS_SPLIT, "slot_c"), (TS_SPLIT, T // P - TS_SPLIT, "slot_e")):
+            rows = keep.tile([P, count], F32, name="ts_rows%d" % first, tag=tag, align_bytes=64)
+            nc.scalar.dma_start(out=rows[:], in_=ts[0].rearrange("(p c) -> p c", p=P)[:, first : first + count])
+            for c in range(count):
+                ts_columns[first + c] = rows[:, c : c + 1]
 
         word_windows = {}
         w1_raw = {}
@@ -72,7 +77,7 @@ def tile_list_tabts_silu_kernel(
         load_w1(0, "slot_b")
         load_w1(1, "slot_d")
 
-        identity = keep.tile([P, P], F32, name="identity")
+        identity = keep.tile([P, P], F32, name="identity", tag="slot_f", align_bytes=64)
         make_identity(nc, identity[:])
 
         w2_codes = keep.tile([P, 2 * M], U8, name="w2_codes", align_bytes=64)
@@ -95,7 +100,7 @@ def tile_list_tabts_silu_kernel(
             spread = psum.tile([P, 4, P], F32, name="spread", tag="bank")
             for i in range(4):
                 nc.tensor.transpose(
-                    spread[:, i, :], ts_rows[:, c0 + i : c0 + i + 1].to_broadcast([P, P]), identity[:]
+                    spread[:, i, :], ts_columns[c0 + i].to_broadcast([P, P]), identity[:]
                 )
             nc.scalar.copy(out=ts_view[:, :, c0 : c0 + 4], in_=spread[:].rearrange("p i n -> p n i"))
 
@@ -125,11 +130,11 @@ def tile_list_tabts_silu_kernel(
                 early_words[(a, half)] = words
 
         load_words(1, "slot_c")
+        load_w1(2, "slot_e")
+        load_words(2, "slot_f")
         gather_early(0)
         quantise_w1(0, "g0")
-        load_w1(2, "slot_b")
         quantise_w1(1, "g1")
-        load_words(2, "slot_d")
         gather_early(1)
         quantise_w1(2, "g2")
 
@@ -137,7 +142,7 @@ def tile_list_tabts_silu_kernel(
         ts_slices = {}
 
         def gather_ts(n):
-            picked = ring.tile([P, TS_SLICE], F32, name="ts_picked", bufs=2)
+            picked = ring.tile([P, TS_SLICE], F32, name="ts_picked", bufs=4)
             nc.vector.tensor_copy(picked[:], ts_window[:].indirect(entries(n * TS_SLICE, TS_SLICE)))
             ts_slices[n] = picked
 
@@ -203,13 +208,13 @@ def tile_list_tabts_silu_kernel(
                 out=out.rearrange("(u p) j -> p u j", p=P)[:, :, g * GROUP : (g + 1) * GROUP], in_=result[:]
             )
 
-        gather_ts(0)
-        gather_ts(1)
+        for g in range(4):
+            gather_ts(g)
         for g in range(AHEAD):
             first_product(g)
         for g in range(GROUPS):
             if g + AHEAD < GROUPS:
                 first_product(g + AHEAD)
             second_product(g)
-            if g + 2 < GROUPS:
-                gather_ts(g + 2)
+            if g + 4 < GROUPS:
+                gather_ts(g + 4)

from contextlib import ExitStack

import concourse.mybir as mybir
from concourse.masks import make_identity

K, H, M, T, S = 1536, 512, 256, 4096, 2048
FLOPS = 2 * K * H * S + 2 * H * M * S

F32 = mybir.dt.float32
BF16 = mybir.dt.bfloat16
I32 = mybir.dt.int32
U32 = mybir.dt.uint32
U16 = mybir.dt.uint16
U8 = mybir.dt.uint8
FP8X4 = mybir.dt.float8_e4m3fn_x4
FP4X4 = mybir.dt.float4_e2m1fn_x4
ACT = mybir.ActivationFunctionType
ALU = mybir.AluOpType

P = 128
PACK = 4
PASSES = K // (P * PACK)
BANK = 128
GROUP = 256
GROUPS = S // GROUP
TS_SLICE = 256
TS_SPLIT = 24
AHEAD = 2


def tile_list_tabts_silu_kernel(
    tc, tab_words, tab_scales, w1, w2_words, w2_scales, ts, b, offs, out
):
    nc = tc.nc
    with ExitStack() as ctx:
        keep = ctx.enter_context(tc.tile_pool(name="keep", bufs=1))
        ring = ctx.enter_context(tc.tile_pool(name="ring", bufs=3))
        psum = ctx.enter_context(tc.psum_pool(name="psum", bufs=8))

        offsets = keep.tile([P, S // 16], U16, name="offsets")
        nc.sync.dma_start(offsets[:], offs)

        def entries(first, count):
            return offsets[:, first // 16 : (first + count) // 16]

        scale_window = keep.tile([P, T], U8, name="scale_window", align_bytes=64)
        w2_plane = keep.tile([P, M], U8, name="w2_plane", align_bytes=64)
        nc.vector.memset(scale_window[:].bitcast(I32), 0)
        nc.vector.memset(w2_plane[:].bitcast(I32), 0)
        for q in range(4):
            nc.gpsimd.dma_start(
                out=scale_window[32 * q : 32 * q + 4 * PASSES, :].bitcast(I32),
                in_=tab_scales[:, 4 * q : 4 * q + 4, :].bitcast(I32),
            )
        ts_columns = {}
        for first, count, tag in ((0, TS_SPLIT, "slot_c"), (TS_SPLIT, T // P - TS_SPLIT, "slot_e")):
            rows = keep.tile([P, count], F32, name="ts_rows%d" % first, tag=tag, align_bytes=64)
            nc.scalar.dma_start(out=rows[:], in_=ts[0].rearrange("(p c) -> p c", p=P)[:, first : first + count])
            for c in range(count):
                ts_columns[first + c] = rows[:, c : c + 1]

        word_windows = {}
        w1_raw = {}

        def load_words(a, tag):
            window = keep.tile([P, T], I32, name="word_window%d" % a, tag=tag, align_bytes=64)
            nc.sync.dma_start(out=window[:], in_=tab_words[a].rearrange("p t i -> p (t i)").bitcast(I32))
            word_windows[a] = window

        def load_w1(a, tag):
            raw = keep.tile([P, PACK, H], F32, name="w1_raw%d" % a, tag=tag, align_bytes=64)
            rows = w1[a * P * PACK : (a + 1) * P * PACK, :]
            nc.sync.dma_start(out=raw[:], in_=rows.rearrange("(p j) c -> p j c", j=PACK))
            w1_raw[a] = raw

        load_words(0, "slot_a")
        load_w1(0, "slot_b")
        load_w1(1, "slot_d")

        identity = keep.tile([P, P], F32, name="identity", tag="slot_f", align_bytes=64)
        make_identity(nc, identity[:])

        w2_codes = keep.tile([P, 2 * M], U8, name="w2_codes", align_bytes=64)
        bias = keep.tile([P, M // P], F32, name="bias")
        nc.scalar.dma_start(out=w2_codes[:].bitcast(I32), in_=w2_words[0].bitcast(I32))
        for q in range(4):
            nc.gpsimd.dma_start(
                out=w2_plane[32 * q : 32 * q + 4, :].bitcast(I32),
                in_=w2_scales[0, 4 * q : 4 * q + 4, :].bitcast(I32),
            )
        with nc.allow_non_contiguous_dma(reason="one bias value a partition"):
            nc.scalar.dma_start(out=bias[:], in_=b.rearrange("(u p) -> p u", p=P))

        tab_planes = keep.tile([P, S], U8, name="tab_planes", align_bytes=64)
        nc.vector.tensor_copy(tab_planes[:], scale_window[:].indirect(offsets[:]))

        ts_window = keep.tile([P, T], F32, name="ts_window", align_bytes=64)
        ts_view = ts_window[:].rearrange("p (n c) -> p n c", n=P)
        for c0 in range(0, T // P, 4):
            spread = psum.tile([P, 4, P], F32, name="spread", tag="bank")
            for i in range(4):
                nc.tensor.transpose(
                    spread[:, i, :], ts_columns[c0 + i].to_broadcast([P, P]), identity[:]
                )
            nc.scalar.copy(out=ts_view[:, :, c0 : c0 + 4], in_=spread[:].rearrange("p i n -> p n i"))

        w1_codes = []
        w1_planes = []

        def quantise_w1(a, tag):
            grouped = keep.tile([P, PACK * H], BF16, name="w1_grouped%d" % a, tag=tag, align_bytes=64)
            nc.scalar.copy(
                out=grouped[:].rearrange("p (t m j) -> p m j t", t=PACK, j=PACK),
                in_=w1_raw[a][:].rearrange("p j (m t) -> p m j t", t=PACK),
            )
            codes = keep.tile([P, H], U32, name="w1_codes%d" % a, align_bytes=64)
            plane = keep.tile([P, H], U8, name="w1_plane%d" % a, align_bytes=64)
            nc.vector.quantize_mx(out=codes[:].bitcast(FP8X4), scales=plane[:], in_=grouped[:])
            w1_codes.append(codes)
            w1_planes.append(plane)

        early_words = {}

        def gather_early(a):
            for half in range(2):
                words = keep.tile([P, S // 2], U32, name="early_words%d_%d" % (a, half), align_bytes=64)
                nc.vector.tensor_copy(
                    words[:], word_windows[a][:].bitcast(U32).indirect(entries(half * S // 2, S // 2))
                )
                early_words[(a, half)] = words

        load_words(1, "slot_c")
        load_w1(2, "slot_e")
        load_words(2, "slot_f")
        gather_early(0)
        quantise_w1(0, "g0")
        quantise_w1(1, "g1")
        gather_early(1)
        quantise_w1(2, "g2")

        h_tiles = {}
        ts_slices = {}

        def gather_ts(n):
            picked = ring.tile([P, TS_SLICE], F32, name="ts_picked", bufs=4)
            nc.vector.tensor_copy(picked[:], ts_window[:].indirect(entries(n * TS_SLICE, TS_SLICE)))
            ts_slices[n] = picked

        def first_product(g):
            last_words = ring.tile([P, GROUP], U32, name="last_words", bufs=4, align_bytes=64)
            nc.vector.tensor_copy(
                last_words[:], word_windows[PASSES - 1][:].bitcast(U32).indirect(entries(g * GROUP, GROUP))
            )
            h_bf16 = ring.tile([P, GROUP, PACK], BF16, name="h_bf16", bufs=4, align_bytes=64)
            for half in range(GROUP // BANK):
                first = g * GROUP + half * BANK
                h_sums = psum.tile([P, PACK, BANK], F32, name="h_sums", tag="bank")
                for a in range(PASSES):
                    if a < PASSES - 1:
                        place = first % (S // 2)
                        words = early_words[(a, first // (S // 2))][:, place : place + BANK]
                    else:
                        words = last_words[:, half * BANK : (half + 1) * BANK]
                    for t in range(PACK):
                        nc.tensor.matmul_mx(
                            out=h_sums[:, t, :],
                            lhsT=w1_codes[a][:, t * P : (t + 1) * P].bitcast(FP8X4),
                            lhsT_scale=w1_planes[a][:, t * P : (t + 1) * P],
                            rhs=words.bitcast(FP8X4),
                            rhs_scale=tab_planes[4 * a : P, first : first + BANK],
                            start=(a == 0 and t == 0),
                            stop=(a == PASSES - 1 and t == PACK - 1),
                        )
                nc.scalar.activation(
                    out=h_bf16[:, half * BANK : (half + 1) * BANK, :],
                    in_=h_sums[:].rearrange("p t n -> p n t"),
                    func=ACT.Relu,
                )
            h_tiles[g] = h_bf16

        def second_product(g):
            h_codes = ring.tile([P, GROUP], U32, name="h_codes", align_bytes=64)
            h_plane = ring.tile([P, GROUP], U8, name="h_plane", align_bytes=64)
            nc.vector.quantize_mx(
                out=h_codes[:].bitcast(FP8X4), scales=h_plane[:], in_=h_tiles[g][:].rearrange("p n t -> p (n t)")
            )
            y_sums = psum.tile([P, M // P, GROUP], F32, name="y_sums", tag="bank")
            for u in range(M // P):
                nc.tensor.matmul_mx(
                    out=y_sums[:, u, :],
                    lhsT=w2_codes[:, 2 * P * u : 2 * P * (u + 1)].bitcast(FP4X4),
                    lhsT_scale=w2_plane[:, P * u : P * (u + 1)],
                    rhs=h_codes[:].bitcast(FP8X4),
                    rhs_scale=h_plane[:],
                    start=True,
                    stop=True,
                )
            first = (g * GROUP) % TS_SLICE
            picked = ts_slices[g * GROUP // TS_SLICE][:, first : first + GROUP]
            scaled = ring.tile([P, M // P, GROUP], F32, name="scaled")
            nc.vector.tensor_tensor(
                scaled[:], y_sums[:], picked.unsqueeze(1).to_broadcast([P, M // P, GROUP]), ALU.mult
            )
            result = ring.tile([P, M // P, GROUP], F32, name="result")
            for u in range(M // P):
                nc.scalar.activation(out=result[:, u, :], in_=scaled[:, u, :], func=ACT.Silu, bias=bias[:, u : u + 1])
            nc.sync.dma_start(
                out=out.rearrange("(u p) j -> p u j", p=P)[:, :, g * GROUP : (g + 1) * GROUP], in_=result[:]
            )

        for g in range(4):
            gather_ts(g)
        for g in range(AHEAD):
            first_product(g)
        for g in range(GROUPS):
            if g + AHEAD < GROUPS:
                first_product(g + AHEAD)
            second_product(g)
            if g + 4 < GROUPS:
                gather_ts(g + 4)
